import numpy as np, ml_dtypes
CORES = [113,118,241,246]
N = 4
import mx_ref
NC = 128
BF = ml_dtypes.bfloat16
def cut(t, i, w=512):
    return t[:, w * i:w * i + w]
def term(a, B):
    return np.stack([mx_ref.matmul(mx_ref.quantize(cut(a, i)), B) for i in range(4)], axis=2).reshape(128, -1)
def setup_inputs(rng):
    def f(*shape):
        return mx_ref.flush((rng.standard_normal(shape, dtype=np.float32) * np.exp2(rng.integers(-2, 3, shape[:-1] + (1,)))).astype(BF))
    return {"a": f(N, 128, 4 * 512), "b": f(N, 128, 2 * 4 * NC)}
def setup_inputs_blocks(rng):
    d = setup_inputs(rng)
    for k in ("a", "b"): d[k] = mx_ref.spread(d[k], rng, 2)
    return d
def setup_inputs_wide(rng):
    d = setup_inputs(rng)
    for k in ("a", "b"): d[k] = mx_ref.flush((d[k].astype(np.float32) * np.exp2(rng.integers(-4, 5, (N, 1, 1))).astype(np.float32)).astype(BF))
    return d
def setup_inputs_lossless(rng):
    a = np.zeros((N, 128, 4 * 128, 4), np.float32)
    for r in range(N):
        k = rng.integers(0, 512, size=4 * 128)
        a[r, k // 4, np.arange(4 * 128), k % 4] = 1.0
    size = np.tile(np.repeat(2.0 ** rng.integers(-4, 5, size=(1, 1, NC)), 4, axis=2), (1, 1, 2))
    b = rng.integers(-1, 2, size=(N, 128, 2 * 4 * NC)) * size
    return {"a": a.reshape(N, 128, 4 * 512).astype(BF), "b": b.astype(np.float32).astype(BF)}
def reference(a, b):
    T = [term(a[r], mx_ref.quantize(cut(b[r], k, 4 * NC))) for r in range(N) for k in range(2)]
    y = np.zeros((N, 128, 4 * NC), np.float32)
    for c in range(N):
        y[c] = mx_ref.total(T[:2 * c + 2])
    return {"y": y}

@@ -1,0 +1,185 @@
+from concourse.mybir import dt, AluOpType, ActivationFunctionType
+
+NCOL = 128
+W = 4 * NCOL
+BANK = 512
+
+SCRATCH = {
+    "abf": ("sbuf", [128, 4 * W], "bfloat16"),
+    "bbf": ("sbuf", [128, 2 * W], "bfloat16"),
+    "qa": ("sbuf", [128, 4 * NCOL], "float8_e4m3fn_x4"),
+    "sa": ("sbuf", [128, 4 * NCOL], "uint8"),
+    "qb": ("sbuf", [128, 2 * NCOL], "float8_e4m3fn_x4"),
+    "sb": ("sbuf", [128, 2 * NCOL], "uint8"),
+    "ones": ("sbuf", [128, 128], "bfloat16"),
+    "ident": ("sbuf", [128, 128], "bfloat16"),
+    "ebf": ("sbuf", [128, 4 * W], "bfloat16"),
+    "qe": ("sbuf", [128, 4 * NCOL], "float8_e4m3fn_x4"),
+    "se": ("sbuf", [128, 4 * NCOL], "uint8"),
+    "hbf": ("sbuf", [128, W], "bfloat16"),
+    "qh": ("sbuf", [128, NCOL], "float8_e4m3fn_x4"),
+    "sh": ("sbuf", [128, NCOL], "uint8"),
+    "pbf": ("sbuf", [128, W], "bfloat16"),
+    "qp": ("sbuf", [128, NCOL], "float8_e4m3fn_x4"),
+    "sp": ("sbuf", [128, NCOL], "uint8"),
+    "qm": ("sbuf", [128, NCOL], "float8_e4m3fn_x4"),
+    "sm": ("sbuf", [128, NCOL], "uint8"),
+    "qn": ("sbuf", [128, NCOL], "float8_e4m3fn_x4"),
+    "sn": ("sbuf", [128, NCOL], "uint8"),
+    "ysb": ("sbuf", [128, W], "float32"),
+    "ps": ("psum", [128, 8 * BANK], "float32"),
+}
+SEMAPHORES = ["ld_b", "ld_a0", "ld_a1", "ones_", "zero_", "ident_", "ecopy", "qe_", "qb_", "qa0", "qa1", "qa2", "qa3",
+              "mm0", "mm1", "mm2", "mm3", "hs", "hv", "qh_", "dm0", "dm1", "dm2", "dm3", "ps_", "pv", "qp_",
+              "arr_m", "arr_n", "ys", "yv", "st", "sent"]
+
+
+def _bits(mask):
+    return [e for e in range(mask.bit_length()) if mask >> e & 1]
+
+
+def _same_chip(topo, a, b):
+    return topo.host(a) == topo.host(b) and topo.chip(a) == topo.chip(b)
+
+
+def _engines(topo, src, dst):
+    mask = topo.mask(src, dst)
+    if _same_chip(topo, src, dst):
+        mask = sum(1 << e for e in _bits(mask)[::2])
+    return mask
+
+
+def rank_program(g, core, T, topo):
+    rank = T.rank_of(core)
+    if rank is None:
+        return
+    sem = T.sem
+    cores = T.cores
+    copy = ActivationFunctionType.Copy
+    v, s, t = g.vector, g.scalar, g.tensor
+
+    def bank(i):
+        return T.ps[:, BANK * i:BANK * i + NCOL]
+
+    def send(dst, codes, plane, to_codes, to_plane, arr):
+        rid, pid = topo.addr(dst, core)
+        mask = _engines(topo, core, dst)
+        g.remote_dma(to_codes[:, 0:NCOL].bitcast(dt.uint8), codes[:, 0:NCOL].bitcast(dt.uint8), arr, sem.sent, pid, rid, mask)
+        g.remote_dma(to_plane[:, 0:NCOL], plane[:, 0:NCOL], arr, sem.sent, pid, rid, mask)
+        return 2 * len(_bits(mask))
+
+    def arrival(src):
+        return 2 * len(_bits(_engines(topo, src, core)))
+
+    half = 2 * W
+    g.sync.dma_start(T.bbf[:, :], T.b[:, :]).then_inc(sem.ld_b, 16)
+    s.dma_start(T.abf[:, 0:half], T.a[:, 0:half]).then_inc(sem.ld_a0, 16)
+    g.sync.dma_start(T.abf[:, half:2 * half], T.a[:, half:2 * half]).then_inc(sem.ld_a1, 16)
+
+    if rank > 0:
+        v.memset(T.ones[:, :], 1.0).then_inc(sem.ones_, 1)
+        v.memset(T.ebf[:, :], 0.0).then_inc(sem.zero_, 1)
+        g.wait_ge(sem.ones_, 1)
+        g.affine_select(T.ident[:, :], T.ones[:, :], [[-1, 128]], AluOpType.is_equal, 0.0, 0, 1).then_inc(sem.ident_, 1)
+        v.wait_ge(sem.zero_, 1)
+        v.wait_ge(sem.ident_, 1)
+        for i in range(4):
+            v.tensor_copy(T.ebf[:, W * i + i:W * (i + 1):4], T.ident[:, :]).then_inc(sem.ecopy, 1)
+
+    v.wait_ge(sem.ld_b, 16)
+    v.quantize_mx(T.qb[:, :], T.sb[:, :], T.bbf[:, :]).then_inc(sem.qb_, 1)
+    for i in range(4):
+        if i % 2 == 0:
+            v.wait_ge(sem["ld_a%d" % (i // 2)], 16)
+        c = slice(NCOL * i, NCOL * (i + 1))
+        v.quantize_mx(T.qa[:, c], T.sa[:, c], T.abf[:, W * i:W * (i + 1)]).then_inc(sem["qa%d" % i], 1)
+
+    last = rank == 3
+    acc = 4 if rank in (1, 2) else 0
+
+    def products(i, to, close):
+        c = slice(NCOL * i, NCOL * (i + 1))
+        for k in range(2):
+            d = slice(NCOL * k, NCOL * (k + 1))
+            m = t.matmul_mx(bank(to), T.qa[:, c], T.sa[:, c], T.qb[:, d], T.sb[:, d], k == 0, k == 1 and close)
+            if k == 1 and close:
+                m.then_inc(sem["mm%d" % i], 1)
+
+    t.wait_ge(sem.qb_, 1)
+    for i in range(4):
+        t.wait_ge(sem["qa%d" % i], 1)
+        products(i, i, not last)
+    if acc:
+        for i in range(4):
+            products(i, acc + i, False)
+
+    if not last:
+        for i in range(3):
+            s.wait_ge(sem["mm%d" % i], 1)
+            s.activation(T.hbf[:, i:W:4], bank(i), copy).then_inc(sem.hs, 1)
+        v.wait_ge(sem.mm3, 1)
+        v.tensor_copy(T.hbf[:, 3:W:4], bank(3)).then_inc(sem.hv, 1)
+        v.wait_ge(sem.hs, 3)
+        v.wait_ge(sem.hv, 1)
+        v.quantize_mx(T.qh[:, :], T.sh[:, :], T.hbf[:, :]).then_inc(sem.qh_, 1)
+    if rank > 0:
+        v.wait_ge(sem.ecopy, 4)
+        v.quantize_mx(T.qe[:, :], T.se[:, :], T.ebf[:, :]).then_inc(sem.qe_, 1)
+
+    def decode(codes, plane, close):
+        for i in range(4):
+            c = slice(NCOL * i, NCOL * (i + 1))
+            m = t.matmul_mx(bank(acc + i), T.qe[:, c], T.se[:, c], codes[:, :], plane[:, :], False, close)
+            if close:
+                m.then_inc(sem["dm%d" % i], 1)
+
+    sent = 0
+    if not last:
+        g.wait_ge(sem.qh_, 1)
+    if rank == 0:
+        sent += send(cores[1], T.qh, T.sh, T.qm, T.sm, sem.arr_m)
+        sent += send(cores[2], T.qh, T.sh, T.qm, T.sm, sem.arr_m)
+    elif rank == 1:
+        sent += send(cores[2], T.qh, T.sh, T.qn, T.sn, sem.arr_n)
+    elif rank == 2:
+        sent += send(cores[3], T.qh, T.sh, T.qn, T.sn, sem.arr_n)
+
+    if rank > 0:
+        t.wait_ge(sem.qe_, 1)
+        if rank > 1:
+            t.wait_ge(sem.arr_n, arrival(cores[1 if rank == 2 else 2]))
+            decode(T.qn, T.sn, False)
+        t.wait_ge(sem.arr_m, arrival(cores[1 if rank == 3 else 0]))
+        decode(T.qm, T.sm, True)
+
+    if rank == 1:
+        s.wait_ge(sem.dm0, 1)
+        s.activation(T.pbf[:, 0:W:4], bank(acc + 0), copy).then_inc(sem.ps_, 1)
+        s.wait_ge(sem.dm2, 1)
+        s.activation(T.pbf[:, 2:W:4], bank(acc + 2), copy).then_inc(sem.ps_, 1)
+        v.wait_ge(sem.dm1, 1)
+        v.tensor_copy(T.pbf[:, 1:W:4], bank(acc + 1)).then_inc(sem.pv, 1)
+        v.wait_ge(sem.dm3, 1)
+        v.tensor_copy(T.pbf[:, 3:W:4], bank(acc + 3)).then_inc(sem.pv, 1)
+        v.wait_ge(sem.ps_, 2)
+        v.wait_ge(sem.pv, 2)
+        v.quantize_mx(T.qp[:, :], T.sp[:, :], T.pbf[:, :]).then_inc(sem.qp_, 1)
+        g.wait_ge(sem.qp_, 1)
+        sent += send(cores[3], T.qp, T.sp, T.qm, T.sm, sem.arr_m)
+
+    on_scalar = (0, 1, 2) if rank == 0 else (0, 2)
+    on_vector = (3,) if rank == 0 else (1, 3)
+    for i in on_scalar:
+        if rank > 1:
+            s.wait_ge(sem["dm%d" % i], 1)
+        s.activation(T.ysb[:, i:W:4], bank(acc + i), copy).then_inc(sem.ys, 1)
+    for i in on_vector:
+        if rank > 1:
+            v.wait_ge(sem["dm%d" % i], 1)
+        v.tensor_copy(T.ysb[:, i:W:4], bank(acc + i)).then_inc(sem.yv, 1)
+    g.sync.wait_ge(sem.ys, len(on_scalar))
+    g.sync.wait_ge(sem.yv, len(on_vector))
+    g.sync.dma_start(T.y[:, :], T.ysb[:, :]).then_inc(sem.st, 16)
+    g.sync.wait_ge(sem.st, 16)
+    if sent:
+        g.wait_ge(sem.sent, sent)

@@ -31,22 +31,11 @@ SCRATCH = {
 }
 SEMAPHORES = ["ld_b", "ld_a0", "ld_a1", "ones_", "zero_", "ident_", "ecopy", "qe_", "qb_", "qa0", "qa1", "qa2", "qa3",
               "mm0", "mm1", "mm2", "mm3", "hs", "hv", "qh_", "dm0", "dm1", "dm2", "dm3", "ps_", "pv", "qp_",
-              "arr_m", "arr_n", "ys", "yv", "st", "sent"]
+              "arr_e", "arr_m", "arr_n", "ys", "yv", "st", "sent"]
 
 
-def _bits(mask):
-    return [e for e in range(mask.bit_length()) if mask >> e & 1]
-
-
-def _same_chip(topo, a, b):
-    return topo.host(a) == topo.host(b) and topo.chip(a) == topo.chip(b)
-
-
-def _engines(topo, src, dst):
-    mask = topo.mask(src, dst)
-    if _same_chip(topo, src, dst):
-        mask = sum(1 << e for e in _bits(mask)[::2])
-    return mask
+def _engines(mask):
+    return bin(mask).count("1")
 
 
 def rank_program(g, core, T, topo):
@@ -63,28 +52,41 @@ def rank_program(g, core, T, topo):
 
     def send(dst, codes, plane, to_codes, to_plane, arr):
         rid, pid = topo.addr(dst, core)
-        mask = _engines(topo, core, dst)
+        mask = topo.mask(core, dst)
         g.remote_dma(to_codes[:, 0:NCOL].bitcast(dt.uint8), codes[:, 0:NCOL].bitcast(dt.uint8), arr, sem.sent, pid, rid, mask)
         g.remote_dma(to_plane[:, 0:NCOL], plane[:, 0:NCOL], arr, sem.sent, pid, rid, mask)
-        return 2 * len(_bits(mask))
+        return 2 * _engines(mask)
 
     def arrival(src):
-        return 2 * len(_bits(_engines(topo, src, core)))
+        return 2 * _engines(topo.mask(src, core))
 
     half = 2 * W
     g.sync.dma_start(T.bbf[:, :], T.b[:, :]).then_inc(sem.ld_b, 16)
     s.dma_start(T.abf[:, 0:half], T.a[:, 0:half]).then_inc(sem.ld_a0, 16)
     g.sync.dma_start(T.abf[:, half:2 * half], T.a[:, half:2 * half]).then_inc(sem.ld_a1, 16)
 
-    if rank > 0:
-        v.memset(T.ones[:, :], 1.0).then_inc(sem.ones_, 1)
-        v.memset(T.ebf[:, :], 0.0).then_inc(sem.zero_, 1)
-        g.wait_ge(sem.ones_, 1)
-        g.affine_select(T.ident[:, :], T.ones[:, :], [[-1, 128]], AluOpType.is_equal, 0.0, 0, 1).then_inc(sem.ident_, 1)
-        v.wait_ge(sem.zero_, 1)
-        v.wait_ge(sem.ident_, 1)
-        for i in range(4):
-            v.tensor_copy(T.ebf[:, W * i + i:W * (i + 1):4], T.ident[:, :]).then_inc(sem.ecopy, 1)
+    mine = (range(0, 1), range(1, 4), range(0, 4), range(0, 4))[rank]
+    ec = slice(NCOL * mine[0], NCOL * (mine[-1] + 1))
+    ew = slice(W * mine[0], W * (mine[-1] + 1))
+
+    def quantise_e():
+        v.wait_ge(sem.ecopy, len(mine))
+        v.quantize_mx(T.qe[:, ec], T.se[:, ec], T.ebf[:, ew]).then_inc(sem.qe_, 1)
+
+    v.memset(T.ones[:, :], 1.0).then_inc(sem.ones_, 1)
+    v.memset(T.ebf[:, ew], 0.0).then_inc(sem.zero_, 1)
+    g.wait_ge(sem.ones_, 1)
+    g.affine_select(T.ident[:, :], T.ones[:, :], [[-1, 128]], AluOpType.is_equal, 0.0, 0, 1).then_inc(sem.ident_, 1)
+    v.wait_ge(sem.zero_, 1)
+    v.wait_ge(sem.ident_, 1)
+    for i in mine:
+        v.tensor_copy(T.ebf[:, W * i + i:W * (i + 1):4], T.ident[:, :]).then_inc(sem.ecopy, 1)
+    sent = 0
+    if rank == 0:
+        quantise_e()
+        g.wait_ge(sem.qe_, 1)
+        g.wait_ge(sem.ld_b, 16)
+        sent += send(cores[1], T.qe, T.se, T.qe, T.se, sem.arr_e)
 
     v.wait_ge(sem.ld_b, 16)
     v.quantize_mx(T.qb[:, :], T.sb[:, :], T.bbf[:, :]).then_inc(sem.qb_, 1)
@@ -123,8 +125,7 @@ def rank_program(g, core, T, topo):
         v.wait_ge(sem.hv, 1)
         v.quantize_mx(T.qh[:, :], T.sh[:, :], T.hbf[:, :]).then_inc(sem.qh_, 1)
     if rank > 0:
-        v.wait_ge(sem.ecopy, 4)
-        v.quantize_mx(T.qe[:, :], T.se[:, :], T.ebf[:, :]).then_inc(sem.qe_, 1)
+        quantise_e()
 
     def decode(codes, plane, close):
         for i in range(4):
@@ -133,7 +134,6 @@ def rank_program(g, core, T, topo):
             if close:
                 m.then_inc(sem["dm%d" % i], 1)
 
-    sent = 0
     if not last:
         g.wait_ge(sem.qh_, 1)
     if rank == 0:
@@ -146,7 +146,9 @@ def rank_program(g, core, T, topo):
 
     if rank > 0:
         t.wait_ge(sem.qe_, 1)
-        if rank > 1:
+        if rank == 1:
+            t.wait_ge(sem.arr_e, arrival(cores[0]))
+        else:
             t.wait_ge(sem.arr_n, arrival(cores[1 if rank == 2 else 2]))
             decode(T.qn, T.sn, False)
         t.wait_ge(sem.arr_m, arrival(cores[1 if rank == 3 else 0]))

@@ -1,8 +1,20 @@
+from concourse.bass import DstId, RemoteDMATransfer
 from concourse.mybir import dt, AluOpType, ActivationFunctionType
 
 NCOL = 128
 W = 4 * NCOL
+HC = NCOL // 2
+HW = W // 2
 BANK = 512
+SLOTS = 3
+
+E_MADE = ((3, None), (0, (128, 448)), (3, (32, 384)), (None, (0, 512)))
+E_SENT = {0: (1, 480, 512), 1: (2, 0, 32), 2: (1, 448, 480)}
+
+
+def _slot(k):
+    return NCOL + k * (HC + NCOL)
+
 
 SCRATCH = {
     "abf": ("sbuf", [128, 4 * W], "bfloat16"),
@@ -19,19 +31,22 @@ SCRATCH = {
     "hbf": ("sbuf", [128, W], "bfloat16"),
     "qh": ("sbuf", [128, NCOL], "float8_e4m3fn_x4"),
     "sh": ("sbuf", [128, NCOL], "uint8"),
-    "pbf": ("sbuf", [128, W], "bfloat16"),
-    "qp": ("sbuf", [128, NCOL], "float8_e4m3fn_x4"),
-    "sp": ("sbuf", [128, NCOL], "uint8"),
+    "hx": ("sbuf", [128, 3 * HW], "bfloat16"),
+    "qf": ("sbuf", [128, NCOL], "float8_e4m3fn_x4"),
+    "sf": ("sbuf", [128, NCOL], "uint8"),
+    "ql": ("sbuf", [128, NCOL], "float8_e4m3fn_x4"),
+    "sl": ("sbuf", [128, NCOL], "uint8"),
     "qm": ("sbuf", [128, NCOL], "float8_e4m3fn_x4"),
     "sm": ("sbuf", [128, NCOL], "uint8"),
-    "qn": ("sbuf", [128, NCOL], "float8_e4m3fn_x4"),
-    "sn": ("sbuf", [128, NCOL], "uint8"),
+    "qx": ("sbuf", [128, _slot(SLOTS)], "float8_e4m3fn_x4"),
+    "sx": ("sbuf", [128, _slot(SLOTS)], "uint8"),
     "ysb": ("sbuf", [128, W], "float32"),
     "ps": ("psum", [128, 8 * BANK], "float32"),
 }
-SEMAPHORES = ["ld_b", "ld_a0", "ld_a1", "ones_", "zero_", "ident_", "ecopy", "qe_", "qb_", "qa0", "qa1", "qa2", "qa3",
-              "mm0", "mm1", "mm2", "mm3", "hs", "hv", "qh_", "dm0", "dm1", "dm2", "dm3", "ps_", "pv", "qp_",
-              "arr_e", "arr_m", "arr_n", "ys", "yv", "st", "sent"]
+SEMAPHORES = ["ld_b", "ld_a0", "ld_a1", "ones_", "zero_a", "zero_b", "pad_", "zq", "ident_", "ecopy_a", "ecopy_b", "qe_a", "qe_b",
+              "qb_", "qa0", "qa1", "qa2", "qa3", "mm0", "mm1", "mm2", "mm3", "hs", "hv", "fs", "fv", "ls", "lv",
+              "qh_", "qf_", "ql_", "dm0", "dm1", "dm2", "dm3", "arr_e", "arr_0", "arr_1f", "arr_1l", "arr_2l", "arr_p",
+              "ys", "yv", "st", "sent"]
 
 
 def _engines(mask):
@@ -46,60 +61,101 @@ def rank_program(g, core, T, topo):
     cores = T.cores
     copy = ActivationFunctionType.Copy
     v, s, t = g.vector, g.scalar, g.tensor
+    sent = [0]
 
-    def bank(i):
-        return T.ps[:, BANK * i:BANK * i + NCOL]
+    def bank(i, lo=0, n=NCOL):
+        return T.ps[:, BANK * i + lo:BANK * i + lo + n]
 
-    def send(dst, codes, plane, to_codes, to_plane, arr):
-        rid, pid = topo.addr(dst, core)
-        mask = topo.mask(core, dst)
-        g.remote_dma(to_codes[:, 0:NCOL].bitcast(dt.uint8), codes[:, 0:NCOL].bitcast(dt.uint8), arr, sem.sent, pid, rid, mask)
-        g.remote_dma(to_plane[:, 0:NCOL], plane[:, 0:NCOL], arr, sem.sent, pid, rid, mask)
-        return 2 * _engines(mask)
+    def way(src, dst, beside=None):
+        m = topo.mask(src, dst)
+        return m if beside is None else m & ~topo.mask(src, beside)
 
-    def arrival(src):
-        return 2 * _engines(topo.mask(src, core))
+    def send(ways, codes, plane, c, to_codes, to_plane, d, n, arr):
+        for out, to in ((codes[:, c:c + n].bitcast(dt.uint8), to_codes[:, d:d + n].bitcast(dt.uint8)),
+                        (plane[:, c:c + n], to_plane[:, d:d + n])):
+            if len(ways) == 1:
+                dst, m = ways[0]
+                rid, pid = topo.addr(dst, core)
+                g.remote_dma(to, out, arr, sem.sent, pid, rid, m)
+            else:
+                transfers = []
+                for dst, m in ways:
+                    rid, pid = topo.addr(dst, core)
+                    transfers.append(RemoteDMATransfer(dst_ids=[DstId(rid=rid, pnc=pid)], dma_engine_mask=m, remote_sem=arr,
+                                                       src=out, dst=to))
+                g.remote_dma_fused(transfers, local_sem=sem.sent)
+        sent[0] += sum(2 * _engines(m) for dst, m in ways)
+
+    def arrival(src, beside=None):
+        return 2 * _engines(way(src, core, beside))
 
     half = 2 * W
     g.sync.dma_start(T.bbf[:, :], T.b[:, :]).then_inc(sem.ld_b, 16)
     s.dma_start(T.abf[:, 0:half], T.a[:, 0:half]).then_inc(sem.ld_a0, 16)
     g.sync.dma_start(T.abf[:, half:2 * half], T.a[:, half:2 * half]).then_inc(sem.ld_a1, 16)
 
-    mine = (range(0, 1), range(1, 4), range(0, 4), range(0, 4))[rank]
-    ec = slice(NCOL * mine[0], NCOL * (mine[-1] + 1))
-    ew = slice(W * mine[0], W * (mine[-1] + 1))
-
-    def quantise_e():
-        v.wait_ge(sem.ecopy, len(mine))
-        v.quantize_mx(T.qe[:, ec], T.se[:, ec], T.ebf[:, ew]).then_inc(sem.qe_, 1)
-
+    first, rest = E_MADE[rank]
+    halves = (0, 0, 2, 3)[rank]
     v.memset(T.ones[:, :], 1.0).then_inc(sem.ones_, 1)
-    v.memset(T.ebf[:, ew], 0.0).then_inc(sem.zero_, 1)
+    if first is not None:
+        v.memset(T.ebf[:, W * first:W * (first + 1)], 0.0).then_inc(sem.zero_a, 1)
+    if rest:
+        v.memset(T.ebf[:, 4 * rest[0]:4 * rest[1]], 0.0).then_inc(sem.zero_b, 1)
     g.wait_ge(sem.ones_, 1)
     g.affine_select(T.ident[:, :], T.ones[:, :], [[-1, 128]], AluOpType.is_equal, 0.0, 0, 1).then_inc(sem.ident_, 1)
-    v.wait_ge(sem.zero_, 1)
-    v.wait_ge(sem.ident_, 1)
-    for i in mine:
-        v.tensor_copy(T.ebf[:, W * i + i:W * (i + 1):4], T.ident[:, :]).then_inc(sem.ecopy, 1)
-    sent = 0
-    if rank == 0:
-        quantise_e()
-        g.wait_ge(sem.qe_, 1)
-        g.wait_ge(sem.ld_b, 16)
-        sent += send(cores[1], T.qe, T.se, T.qe, T.se, sem.arr_e)
 
-    v.wait_ge(sem.ld_b, 16)
-    v.quantize_mx(T.qb[:, :], T.sb[:, :], T.bbf[:, :]).then_inc(sem.qb_, 1)
-    for i in range(4):
+    def diagonal(i, lo, hi, done):
+        s.activation(T.ebf[:, W * i + 4 * lo + i:W * i + 4 * hi:4], T.ident[:, lo:hi], copy).then_inc(done, 1)
+
+    s.wait_ge(sem.ident_, 1)
+    if first is not None:
+        s.wait_ge(sem.zero_a, 1)
+        diagonal(first, 0, NCOL, sem.ecopy_a)
+        v.wait_ge(sem.ecopy_a, 1)
+        c = slice(NCOL * first, NCOL * (first + 1))
+        v.quantize_mx(T.qe[:, c], T.se[:, c], T.ebf[:, W * first:W * (first + 1)]).then_inc(sem.qe_a, 1)
+        to, lo, hi = E_SENT[rank]
+        g.wait_ge(sem.qe_a, 1)
+        send([(cores[to], way(core, cores[to]))], T.qe, T.se, lo, T.qe, T.se, lo, hi - lo, sem.arr_e)
+    if rank in (1, 2):
+        v.memset(T.hx[:, HW:2 * HW], 0.0).then_inc(sem.pad_, 1)
+    if halves:
+        v.wait_ge(sem.zero_b, 1)
+        for k in range(halves + 1):
+            z = slice(_slot(k) - NCOL, _slot(k))
+            v.quantize_mx(T.qx[:, z], T.sx[:, z], T.ebf[:, W:2 * W]).then_inc(sem.zq, 1)
+        s.wait_ge(sem.zq, halves + 1)
+    if rest:
+        s.wait_ge(sem.zero_b, 1)
+        pieces = [(i, max(rest[0] - NCOL * i, 0), min(rest[1] - NCOL * i, NCOL)) for i in range(4)]
+        pieces = [p for p in pieces if p[1] < p[2]]
+        for i, lo, hi in pieces:
+            diagonal(i, lo, hi, sem.ecopy_b)
+
+    def quantise_e():
+        v.wait_ge(sem.ecopy_b, len(pieces))
+        c = slice(rest[0], rest[1])
+        v.quantize_mx(T.qe[:, c], T.se[:, c], T.ebf[:, 4 * rest[0]:4 * rest[1]]).then_inc(sem.qe_b, 1)
+
+    def wait_e():
+        if first is not None:
+            t.wait_ge(sem.qe_a, 1)
+        t.wait_ge(sem.qe_b, 1)
+        n = sum(arrival(cores[r]) for r in E_SENT if E_SENT[r][0] == rank)
+        if n:
+            t.wait_ge(sem.arr_e, n)
+        if halves:
+            t.wait_ge(sem.zq, halves + 1)
+
+    def quantise_a(i):
         if i % 2 == 0:
             v.wait_ge(sem["ld_a%d" % (i // 2)], 16)
         c = slice(NCOL * i, NCOL * (i + 1))
         v.quantize_mx(T.qa[:, c], T.sa[:, c], T.abf[:, W * i:W * (i + 1)]).then_inc(sem["qa%d" % i], 1)
 
-    last = rank == 3
     acc = 4 if rank in (1, 2) else 0
 
-    def products(i, to, close):
+    def product(i, to, close):
         c = slice(NCOL * i, NCOL * (i + 1))
         for k in range(2):
             d = slice(NCOL * k, NCOL * (k + 1))
@@ -107,15 +163,68 @@ def rank_program(g, core, T, topo):
             if k == 1 and close:
                 m.then_inc(sem["mm%d" % i], 1)
 
-    t.wait_ge(sem.qb_, 1)
-    for i in range(4):
-        t.wait_ge(sem["qa%d" % i], 1)
-        products(i, i, not last)
-    if acc:
+    def decode(close):
         for i in range(4):
-            products(i, acc + i, False)
+            c = slice(NCOL * i, NCOL * (i + 1))
+            m = t.matmul_mx(bank(acc + i), T.qe[:, c], T.se[:, c], T.qm[:, :], T.sm[:, :], False, i in close)
+            if i in close:
+                m.then_inc(sem["dm%d" % i], 1)
 
-    if not last:
+    def decode_half(slot, base, to, done=None):
+        for r in range(4):
+            i, h = base + r // 2, r % 2
+            c = slice(NCOL * r, NCOL * (r + 1))
+            d = slice(_slot(slot) - HC * h, _slot(slot) - HC * h + NCOL)
+            close = done is not None and h == 1
+            m = t.matmul_mx(bank(to + i), T.qe[:, c], T.se[:, c], T.qx[:, d], T.sx[:, d], False, close)
+            if close:
+                m.then_inc(sem["%s%d" % (done, i)], 1)
+
+    def half_copy(scalar, i, done):
+        base = 0 if i < 2 else 2 * HW
+        for h in range(2):
+            out = T.hx[:, base + 2 * (i % 2) + h:base + HW:4]
+            if scalar:
+                s.activation(out, bank(i, HC * h, HC), copy).then_inc(done, 1)
+            else:
+                v.tensor_copy(out, bank(i, HC * h, HC)).then_inc(done, 1)
+
+    def first_half():
+        s.wait_ge(sem.mm0, 1)
+        half_copy(True, 0, sem.fs)
+        v.wait_ge(sem.mm1, 1)
+        half_copy(False, 1, sem.fv)
+        v.wait_ge(sem.pad_, 1)
+        v.wait_ge(sem.fs, 2)
+        v.wait_ge(sem.fv, 2)
+        v.quantize_mx(T.qf[:, :], T.sf[:, :], T.hx[:, 0:W]).then_inc(sem.qf_, 1)
+
+    def last_half():
+        s.wait_ge(sem.mm2, 1)
+        half_copy(True, 2, sem.ls)
+        v.wait_ge(sem.mm3, 1)
+        half_copy(False, 3, sem.lv)
+        v.wait_ge(sem.pad_, 1)
+        v.wait_ge(sem.ls, 2)
+        v.wait_ge(sem.lv, 2)
+        v.quantize_mx(T.ql[:, :], T.sl[:, :], T.hx[:, HW:HW + W]).then_inc(sem.ql_, 1)
+
+    def send_half(to, last, slot, arr):
+        q, p, c = (T.ql, T.sl, HC) if last else (T.qf, T.sf, 0)
+        send([(cores[to], way(core, cores[to]))], q, p, c, T.qx, T.sx, _slot(slot), HC, arr)
+
+    v.wait_ge(sem.ld_b, 16)
+    v.quantize_mx(T.qb[:, :], T.sb[:, :], T.bbf[:, :]).then_inc(sem.qb_, 1)
+    quantise_a(0)
+    quantise_a(1)
+    t.wait_ge(sem.qb_, 1)
+
+    if rank == 0:
+        quantise_a(2)
+        quantise_a(3)
+        for i in range(4):
+            t.wait_ge(sem["qa%d" % i], 1)
+            product(i, i, True)
         for i in range(3):
             s.wait_ge(sem["mm%d" % i], 1)
             s.activation(T.hbf[:, i:W:4], bank(i), copy).then_inc(sem.hs, 1)
@@ -124,64 +233,92 @@ def rank_program(g, core, T, topo):
         v.wait_ge(sem.hs, 3)
         v.wait_ge(sem.hv, 1)
         v.quantize_mx(T.qh[:, :], T.sh[:, :], T.hbf[:, :]).then_inc(sem.qh_, 1)
-    if rank > 0:
-        quantise_e()
-
-    def decode(codes, plane, close):
-        for i in range(4):
-            c = slice(NCOL * i, NCOL * (i + 1))
-            m = t.matmul_mx(bank(acc + i), T.qe[:, c], T.se[:, c], codes[:, :], plane[:, :], False, close)
-            if close:
-                m.then_inc(sem["dm%d" % i], 1)
-
-    if not last:
         g.wait_ge(sem.qh_, 1)
-    if rank == 0:
-        sent += send(cores[1], T.qh, T.sh, T.qm, T.sm, sem.arr_m)
-        sent += send(cores[2], T.qh, T.sh, T.qm, T.sm, sem.arr_m)
+        send([(cores[3], way(core, cores[3]))], T.qh, T.sh, 0, T.qm, T.sm, 0, NCOL, sem.arr_0)
+        send([(cores[2], way(core, cores[2])), (cores[1], way(core, cores[1], cores[2]))],
+             T.qh, T.sh, 0, T.qm, T.sm, 0, NCOL, sem.arr_0)
+
     elif rank == 1:
-        sent += send(cores[2], T.qh, T.sh, T.qn, T.sn, sem.arr_n)
+        first_half()
+        quantise_a(2)
+        quantise_a(3)
+        last_half()
+        quantise_e()
+        for i in range(4):
+            t.wait_ge(sem["qa%d" % i], 1)
+            product(i, i, True)
+        for i in range(4):
+            product(i, acc + i, False)
+        wait_e()
+        t.wait_ge(sem.arr_0, arrival(cores[0], cores[2]))
+        decode((0, 1, 2, 3))
+        g.wait_ge(sem.qf_, 1)
+        send_half(2, False, 0, sem.arr_1f)
+        g.wait_ge(sem.ql_, 1)
+        send_half(3, True, 0, sem.arr_1l)
+        send_half(2, True, 1, sem.arr_1l)
+
     elif rank == 2:
-        sent += send(cores[3], T.qh, T.sh, T.qn, T.sn, sem.arr_n)
+        quantise_e()
+        quantise_a(2)
+        quantise_a(3)
+        last_half()
+        first_half()
+        for i in range(2):
+            t.wait_ge(sem["qa%d" % i], 1)
+            product(i, i, False)
+        for i in range(2):
+            product(i, acc + i, False)
+        for i in range(2, 4):
+            t.wait_ge(sem["qa%d" % i], 1)
+            product(i, i, True)
+        for i in range(2, 4):
+            product(i, acc + i, False)
+        wait_e()
+        t.wait_ge(sem.arr_1f, arrival(cores[1]))
+        decode_half(0, 0, 0, "mm")
+        decode_half(0, 0, acc)
+        t.wait_ge(sem.arr_1l, arrival(cores[1]))
+        decode_half(1, 2, acc)
+        t.wait_ge(sem.arr_0, arrival(cores[0]))
+        decode((0, 1, 2, 3))
+        g.wait_ge(sem.ql_, 1)
+        send_half(3, True, 1, sem.arr_2l)
+        g.wait_ge(sem.qf_, 1)
+        send_half(3, False, 2, sem.arr_p)
 
-    if rank > 0:
-        t.wait_ge(sem.qe_, 1)
-        if rank == 1:
-            t.wait_ge(sem.arr_e, arrival(cores[0]))
-        else:
-            t.wait_ge(sem.arr_n, arrival(cores[1 if rank == 2 else 2]))
-            decode(T.qn, T.sn, False)
-        t.wait_ge(sem.arr_m, arrival(cores[1 if rank == 3 else 0]))
-        decode(T.qm, T.sm, True)
+    else:
+        quantise_e()
+        quantise_a(2)
+        quantise_a(3)
+        for i in range(4):
+            t.wait_ge(sem["qa%d" % i], 1)
+            product(i, i, False)
+        wait_e()
+        t.wait_ge(sem.arr_1l, arrival(cores[1]))
+        decode_half(0, 2, acc)
+        t.wait_ge(sem.arr_2l, arrival(cores[2]))
+        decode_half(1, 2, acc)
+        t.wait_ge(sem.arr_0, arrival(cores[0]))
+        decode((2, 3))
+        t.wait_ge(sem.arr_p, arrival(cores[2]))
+        decode_half(2, 0, acc, "dm")
 
-    if rank == 1:
-        s.wait_ge(sem.dm0, 1)
-        s.activation(T.pbf[:, 0:W:4], bank(acc + 0), copy).then_inc(sem.ps_, 1)
-        s.wait_ge(sem.dm2, 1)
-        s.activation(T.pbf[:, 2:W:4], bank(acc + 2), copy).then_inc(sem.ps_, 1)
-        v.wait_ge(sem.dm1, 1)
-        v.tensor_copy(T.pbf[:, 1:W:4], bank(acc + 1)).then_inc(sem.pv, 1)
-        v.wait_ge(sem.dm3, 1)
-        v.tensor_copy(T.pbf[:, 3:W:4], bank(acc + 3)).then_inc(sem.pv, 1)
-        v.wait_ge(sem.ps_, 2)
-        v.wait_ge(sem.pv, 2)
-        v.quantize_mx(T.qp[:, :], T.sp[:, :], T.pbf[:, :]).then_inc(sem.qp_, 1)
-        g.wait_ge(sem.qp_, 1)
-        sent += send(cores[3], T.qp, T.sp, T.qm, T.sm, sem.arr_m)
-
-    on_scalar = (0, 1, 2) if rank == 0 else (0, 2)
-    on_vector = (3,) if rank == 0 else (1, 3)
+    on_scalar = ((0, 1, 2), (0, 2), (0, 2), (2, 0))[rank]
+    on_vector = ((3,), (1, 3), (1, 3), (3, 1))[rank]
     for i in on_scalar:
-        if rank > 1:
+        if rank > 0:
             s.wait_ge(sem["dm%d" % i], 1)
         s.activation(T.ysb[:, i:W:4], bank(acc + i), copy).then_inc(sem.ys, 1)
     for i in on_vector:
-        if rank > 1:
+        if rank > 0:
             v.wait_ge(sem["dm%d" % i], 1)
         v.tensor_copy(T.ysb[:, i:W:4], bank(acc + i)).then_inc(sem.yv, 1)
     g.sync.wait_ge(sem.ys, len(on_scalar))
     g.sync.wait_ge(sem.yv, len(on_vector))
+    if rank == 0:
+        g.sync.wait_ge(sem.sent, sent[0])
     g.sync.dma_start(T.y[:, :], T.ysb[:, :]).then_inc(sem.st, 16)
     g.sync.wait_ge(sem.st, 16)
-    if sent:
-        g.wait_ge(sem.sent, sent)
+    if sent[0]:
+        g.wait_ge(sem.sent, sent[0])

from concourse.bass import DstId, RemoteDMATransfer
from concourse.mybir import dt, AluOpType, ActivationFunctionType

NCOL = 128
W = 4 * NCOL
HC = NCOL // 2
HW = W // 2
BANK = 512
SLOTS = 3

E_MADE = ((3, None), (0, (128, 448)), (3, (32, 384)), (None, (0, 512)))
E_SENT = {0: (1, 480, 512), 1: (2, 0, 32), 2: (1, 448, 480)}


def _slot(k):
    return NCOL + k * (HC + NCOL)


SCRATCH = {
    "abf": ("sbuf", [128, 4 * W], "bfloat16"),
    "bbf": ("sbuf", [128, 2 * W], "bfloat16"),
    "qa": ("sbuf", [128, 4 * NCOL], "float8_e4m3fn_x4"),
    "sa": ("sbuf", [128, 4 * NCOL], "uint8"),
    "qb": ("sbuf", [128, 2 * NCOL], "float8_e4m3fn_x4"),
    "sb": ("sbuf", [128, 2 * NCOL], "uint8"),
    "ones": ("sbuf", [128, 128], "bfloat16"),
    "ident": ("sbuf", [128, 128], "bfloat16"),
    "ebf": ("sbuf", [128, 4 * W], "bfloat16"),
    "qe": ("sbuf", [128, 4 * NCOL], "float8_e4m3fn_x4"),
    "se": ("sbuf", [128, 4 * NCOL], "uint8"),
    "hbf": ("sbuf", [128, W], "bfloat16"),
    "qh": ("sbuf", [128, NCOL], "float8_e4m3fn_x4"),
    "sh": ("sbuf", [128, NCOL], "uint8"),
    "hx": ("sbuf", [128, 3 * HW], "bfloat16"),
    "qf": ("sbuf", [128, NCOL], "float8_e4m3fn_x4"),
    "sf": ("sbuf", [128, NCOL], "uint8"),
    "ql": ("sbuf", [128, NCOL], "float8_e4m3fn_x4"),
    "sl": ("sbuf", [128, NCOL], "uint8"),
    "qm": ("sbuf", [128, NCOL], "float8_e4m3fn_x4"),
    "sm": ("sbuf", [128, NCOL], "uint8"),
    "qx": ("sbuf", [128, _slot(SLOTS)], "float8_e4m3fn_x4"),
    "sx": ("sbuf", [128, _slot(SLOTS)], "uint8"),
    "ysb": ("sbuf", [128, W], "float32"),
    "ps": ("psum", [128, 8 * BANK], "float32"),
}
SEMAPHORES = ["ld_b", "ld_a0", "ld_a1", "ones_", "zero_a", "zero_b", "pad_", "zq", "ident_", "ecopy_a", "ecopy_b", "qe_a", "qe_b",
              "qb_", "qa0", "qa1", "qa2", "qa3", "mm0", "mm1", "mm2", "mm3", "hs", "hv", "fs", "fv", "ls", "lv",
              "qh_", "qf_", "ql_", "dm0", "dm1", "dm2", "dm3", "arr_e", "arr_0", "arr_1f", "arr_1l", "arr_2l", "arr_p",
              "ys", "yv", "st", "sent"]


def _engines(mask):
    return bin(mask).count("1")


def rank_program(g, core, T, topo):
    rank = T.rank_of(core)
    if rank is None:
        return
    sem = T.sem
    cores = T.cores
    copy = ActivationFunctionType.Copy
    v, s, t = g.vector, g.scalar, g.tensor
    sent = [0]

    def bank(i, lo=0, n=NCOL):
        return T.ps[:, BANK * i + lo:BANK * i + lo + n]

    def way(src, dst, beside=None):
        m = topo.mask(src, dst)
        return m if beside is None else m & ~topo.mask(src, beside)

    def send(ways, codes, plane, c, to_codes, to_plane, d, n, arr):
        for out, to in ((codes[:, c:c + n].bitcast(dt.uint8), to_codes[:, d:d + n].bitcast(dt.uint8)),
                        (plane[:, c:c + n], to_plane[:, d:d + n])):
            if len(ways) == 1:
                dst, m = ways[0]
                rid, pid = topo.addr(dst, core)
                g.remote_dma(to, out, arr, sem.sent, pid, rid, m)
            else:
                transfers = []
                for dst, m in ways:
                    rid, pid = topo.addr(dst, core)
                    transfers.append(RemoteDMATransfer(dst_ids=[DstId(rid=rid, pnc=pid)], dma_engine_mask=m, remote_sem=arr,
                                                       src=out, dst=to))
                g.remote_dma_fused(transfers, local_sem=sem.sent)
        sent[0] += sum(2 * _engines(m) for dst, m in ways)

    def arrival(src, beside=None):
        return 2 * _engines(way(src, core, beside))

    half = 2 * W
    g.sync.dma_start(T.bbf[:, :], T.b[:, :]).then_inc(sem.ld_b, 16)
    s.dma_start(T.abf[:, 0:half], T.a[:, 0:half]).then_inc(sem.ld_a0, 16)
    g.sync.dma_start(T.abf[:, half:2 * half], T.a[:, half:2 * half]).then_inc(sem.ld_a1, 16)

    first, rest = E_MADE[rank]
    halves = (0, 0, 2, 3)[rank]
    v.memset(T.ones[:, :], 1.0).then_inc(sem.ones_, 1)
    if first is not None:
        v.memset(T.ebf[:, W * first:W * (first + 1)], 0.0).then_inc(sem.zero_a, 1)
    if rest:
        v.memset(T.ebf[:, 4 * rest[0]:4 * rest[1]], 0.0).then_inc(sem.zero_b, 1)
    g.wait_ge(sem.ones_, 1)
    g.affine_select(T.ident[:, :], T.ones[:, :], [[-1, 128]], AluOpType.is_equal, 0.0, 0, 1).then_inc(sem.ident_, 1)

    def diagonal(i, lo, hi, done):
        s.activation(T.ebf[:, W * i + 4 * lo + i:W * i + 4 * hi:4], T.ident[:, lo:hi], copy).then_inc(done, 1)

    s.wait_ge(sem.ident_, 1)
    if first is not None:
        s.wait_ge(sem.zero_a, 1)
        diagonal(first, 0, NCOL, sem.ecopy_a)
        v.wait_ge(sem.ecopy_a, 1)
        c = slice(NCOL * first, NCOL * (first + 1))
        v.quantize_mx(T.qe[:, c], T.se[:, c], T.ebf[:, W * first:W * (first + 1)]).then_inc(sem.qe_a, 1)
        to, lo, hi = E_SENT[rank]
        g.wait_ge(sem.qe_a, 1)
        send([(cores[to], way(core, cores[to]))], T.qe, T.se, lo, T.qe, T.se, lo, hi - lo, sem.arr_e)
    if rank in (1, 2):
        v.memset(T.hx[:, HW:2 * HW], 0.0).then_inc(sem.pad_, 1)
    if halves:
        v.wait_ge(sem.zero_b, 1)
        for k in range(halves + 1):
            z = slice(_slot(k) - NCOL, _slot(k))
            v.quantize_mx(T.qx[:, z], T.sx[:, z], T.ebf[:, W:2 * W]).then_inc(sem.zq, 1)
        s.wait_ge(sem.zq, halves + 1)
    if rest:
        s.wait_ge(sem.zero_b, 1)
        pieces = [(i, max(rest[0] - NCOL * i, 0), min(rest[1] - NCOL * i, NCOL)) for i in range(4)]
        pieces = [p for p in pieces if p[1] < p[2]]
        for i, lo, hi in pieces:
            diagonal(i, lo, hi, sem.ecopy_b)

    def quantise_e():
        v.wait_ge(sem.ecopy_b, len(pieces))
        c = slice(rest[0], rest[1])
        v.quantize_mx(T.qe[:, c], T.se[:, c], T.ebf[:, 4 * rest[0]:4 * rest[1]]).then_inc(sem.qe_b, 1)

    def wait_e():
        if first is not None:
            t.wait_ge(sem.qe_a, 1)
        t.wait_ge(sem.qe_b, 1)
        n = sum(arrival(cores[r]) for r in E_SENT if E_SENT[r][0] == rank)
        if n:
            t.wait_ge(sem.arr_e, n)
        if halves:
            t.wait_ge(sem.zq, halves + 1)

    def quantise_a(i):
        if i % 2 == 0:
            v.wait_ge(sem["ld_a%d" % (i // 2)], 16)
        c = slice(NCOL * i, NCOL * (i + 1))
        v.quantize_mx(T.qa[:, c], T.sa[:, c], T.abf[:, W * i:W * (i + 1)]).then_inc(sem["qa%d" % i], 1)

    acc = 4 if rank in (1, 2) else 0

    def product(i, to, close):
        c = slice(NCOL * i, NCOL * (i + 1))
        for k in range(2):
            d = slice(NCOL * k, NCOL * (k + 1))
            m = t.matmul_mx(bank(to), T.qa[:, c], T.sa[:, c], T.qb[:, d], T.sb[:, d], k == 0, k == 1 and close)
            if k == 1 and close:
                m.then_inc(sem["mm%d" % i], 1)

    def decode(close):
        for i in range(4):
            c = slice(NCOL * i, NCOL * (i + 1))
            m = t.matmul_mx(bank(acc + i), T.qe[:, c], T.se[:, c], T.qm[:, :], T.sm[:, :], False, i in close)
            if i in close:
                m.then_inc(sem["dm%d" % i], 1)

    def decode_half(slot, base, to, done=None):
        for r in range(4):
            i, h = base + r // 2, r % 2
            c = slice(NCOL * r, NCOL * (r + 1))
            d = slice(_slot(slot) - HC * h, _slot(slot) - HC * h + NCOL)
            close = done is not None and h == 1
            m = t.matmul_mx(bank(to + i), T.qe[:, c], T.se[:, c], T.qx[:, d], T.sx[:, d], False, close)
            if close:
                m.then_inc(sem["%s%d" % (done, i)], 1)

    def half_copy(scalar, i, done):
        base = 0 if i < 2 else 2 * HW
        for h in range(2):
            out = T.hx[:, base + 2 * (i % 2) + h:base + HW:4]
            if scalar:
                s.activation(out, bank(i, HC * h, HC), copy).then_inc(done, 1)
            else:
                v.tensor_copy(out, bank(i, HC * h, HC)).then_inc(done, 1)

    def first_half():
        s.wait_ge(sem.mm0, 1)
        half_copy(True, 0, sem.fs)
        v.wait_ge(sem.mm1, 1)
        half_copy(False, 1, sem.fv)
        v.wait_ge(sem.pad_, 1)
        v.wait_ge(sem.fs, 2)
        v.wait_ge(sem.fv, 2)
        v.quantize_mx(T.qf[:, :], T.sf[:, :], T.hx[:, 0:W]).then_inc(sem.qf_, 1)

    def last_half():
        s.wait_ge(sem.mm2, 1)
        half_copy(True, 2, sem.ls)
        v.wait_ge(sem.mm3, 1)
        half_copy(False, 3, sem.lv)
        v.wait_ge(sem.pad_, 1)
        v.wait_ge(sem.ls, 2)
        v.wait_ge(sem.lv, 2)
        v.quantize_mx(T.ql[:, :], T.sl[:, :], T.hx[:, HW:HW + W]).then_inc(sem.ql_, 1)

    def send_half(to, last, slot, arr):
        q, p, c = (T.ql, T.sl, HC) if last else (T.qf, T.sf, 0)
        send([(cores[to], way(core, cores[to]))], q, p, c, T.qx, T.sx, _slot(slot), HC, arr)

    v.wait_ge(sem.ld_b, 16)
    v.quantize_mx(T.qb[:, :], T.sb[:, :], T.bbf[:, :]).then_inc(sem.qb_, 1)
    quantise_a(0)
    quantise_a(1)
    t.wait_ge(sem.qb_, 1)

    if rank == 0:
        quantise_a(2)
        quantise_a(3)
        for i in range(4):
            t.wait_ge(sem["qa%d" % i], 1)
            product(i, i, True)
        for i in range(3):
            s.wait_ge(sem["mm%d" % i], 1)
            s.activation(T.hbf[:, i:W:4], bank(i), copy).then_inc(sem.hs, 1)
        v.wait_ge(sem.mm3, 1)
        v.tensor_copy(T.hbf[:, 3:W:4], bank(3)).then_inc(sem.hv, 1)
        v.wait_ge(sem.hs, 3)
        v.wait_ge(sem.hv, 1)
        v.quantize_mx(T.qh[:, :], T.sh[:, :], T.hbf[:, :]).then_inc(sem.qh_, 1)
        g.wait_ge(sem.qh_, 1)
        send([(cores[3], way(core, cores[3]))], T.qh, T.sh, 0, T.qm, T.sm, 0, NCOL, sem.arr_0)
        send([(cores[2], way(core, cores[2])), (cores[1], way(core, cores[1], cores[2]))],
             T.qh, T.sh, 0, T.qm, T.sm, 0, NCOL, sem.arr_0)

    elif rank == 1:
        first_half()
        quantise_a(2)
        quantise_a(3)
        last_half()
        quantise_e()
        for i in range(4):
            t.wait_ge(sem["qa%d" % i], 1)
            product(i, i, True)
        for i in range(4):
            product(i, acc + i, False)
        wait_e()
        t.wait_ge(sem.arr_0, arrival(cores[0], cores[2]))
        decode((0, 1, 2, 3))
        g.wait_ge(sem.qf_, 1)
        send_half(2, False, 0, sem.arr_1f)
        g.wait_ge(sem.ql_, 1)
        send_half(3, True, 0, sem.arr_1l)
        send_half(2, True, 1, sem.arr_1l)

    elif rank == 2:
        quantise_e()
        quantise_a(2)
        quantise_a(3)
        last_half()
        first_half()
        for i in range(2):
            t.wait_ge(sem["qa%d" % i], 1)
            product(i, i, False)
        for i in range(2):
            product(i, acc + i, False)
        for i in range(2, 4):
            t.wait_ge(sem["qa%d" % i], 1)
            product(i, i, True)
        for i in range(2, 4):
            product(i, acc + i, False)
        wait_e()
        t.wait_ge(sem.arr_1f, arrival(cores[1]))
        decode_half(0, 0, 0, "mm")
        decode_half(0, 0, acc)
        t.wait_ge(sem.arr_1l, arrival(cores[1]))
        decode_half(1, 2, acc)
        t.wait_ge(sem.arr_0, arrival(cores[0]))
        decode((0, 1, 2, 3))
        g.wait_ge(sem.ql_, 1)
        send_half(3, True, 1, sem.arr_2l)
        g.wait_ge(sem.qf_, 1)
        send_half(3, False, 2, sem.arr_p)

    else:
        quantise_e()
        quantise_a(2)
        quantise_a(3)
        for i in range(4):
            t.wait_ge(sem["qa%d" % i], 1)
            product(i, i, False)
        wait_e()
        t.wait_ge(sem.arr_1l, arrival(cores[1]))
        decode_half(0, 2, acc)
        t.wait_ge(sem.arr_2l, arrival(cores[2]))
        decode_half(1, 2, acc)
        t.wait_ge(sem.arr_0, arrival(cores[0]))
        decode((2, 3))
        t.wait_ge(sem.arr_p, arrival(cores[2]))
        decode_half(2, 0, acc, "dm")

    on_scalar = ((0, 1, 2), (0, 2), (0, 2), (2, 0))[rank]
    on_vector = ((3,), (1, 3), (1, 3), (3, 1))[rank]
    for i in on_scalar:
        if rank > 0:
            s.wait_ge(sem["dm%d" % i], 1)
        s.activation(T.ysb[:, i:W:4], bank(acc + i), copy).then_inc(sem.ys, 1)
    for i in on_vector:
        if rank > 0:
            v.wait_ge(sem["dm%d" % i], 1)
        v.tensor_copy(T.ysb[:, i:W:4], bank(acc + i)).then_inc(sem.yv, 1)
    g.sync.wait_ge(sem.ys, len(on_scalar))
    g.sync.wait_ge(sem.yv, len(on_vector))
    if rank == 0:
        g.sync.wait_ge(sem.sent, sent[0])
    g.sync.dma_start(T.y[:, :], T.ysb[:, :]).then_inc(sem.st, 16)
    g.sync.wait_ge(sem.st, 16)
    if sent[0]:
        g.wait_ge(sem.sent, sent[0])
